import numpy as np
CORES = [0,1,2,3]
N = 4
COUNTS = [[0,1024,256,128],[0,0,0,0],[256,1024,0,0],[0,1024,0,0]]
XW, YW = 1408, 3072
def setup_inputs(rng):
    return {"x": rng.standard_normal((N, 128, XW), dtype=np.float32)}
def reference(x):
    y = np.full((N, 128, YW), np.nan, x.dtype)
    fill = [0] * N
    for s in range(N):
        o = 0
        for d in range(N):
            c = COUNTS[s][d]
            y[d][:, fill[d]:fill[d] + c] = x[s][:, o:o + c]
            o += c; fill[d] += c
    return {"y": y}

N = 4
XW, YW = 1408, 3072
PIECE = 512
MAXK = 2

SCRATCH = {
    "stage": ("sbuf", [128, XW], "float32"),
    "land": ("sbuf", [128, YW], "float32"),
}
SEMAPHORES = (["sent", "stored"]
              + ["ld%d_%d" % (d, k) for d in range(N) for k in range(MAXK)]
              + ["arr%d_%d" % (s, k) for s in range(N) for k in range(MAXK)])


def pieces(width):
    return [(a, min(PIECE, width - a)) for a in range(0, width, PIECE)]


def rank_program(g, core, T, topo):
    me = T.rank_of(core)
    if me is None:
        return
    counts = T.tables["COUNTS"]
    n = len(counts)
    queues = [g.sync, g.scalar]
    turn = [0]

    def next_queue():
        turn[0] += 1
        return queues[turn[0] % 2]

    stores = 0

    own = counts[me][me]
    if own:
        o = sum(counts[me][:me])
        f = sum(counts[s][me] for s in range(me))
        next_queue().dma_start(T.y[:, f:f + own], T.x[:, o:o + own]).then_inc(T.sem.stored, 16)
        stores += 1

    out = []
    for d in sorted(range(n), key=lambda d: -counts[me][d]):
        if d == me:
            continue
        o = sum(counts[me][:d])
        f = sum(counts[s][d] for s in range(me))
        for k, (a, c) in enumerate(pieces(counts[me][d])):
            out.append((d, k, o + a, f + a, c))
    for d, k, o, f, c in out:
        next_queue().dma_start(T.stage[:, o:o + c], T.x[:, o:o + c]).then_inc(T.sem["ld%d_%d" % (d, k)], 16)

    sent = 0
    for d, k, o, f, c in out:
        dst = T.cores[d]
        rid, pid, _se = topo.addr(dst)
        g.wait_ge(T.sem["ld%d_%d" % (d, k)], 16)
        g.remote_dma(out_ap=T.land[:, f:f + c], in_ap=T.stage[:, o:o + c],
                     remote_sem=T.sem["arr%d_%d" % (me, k)], local_sem=T.sem.sent,
                     pid=pid, routing_id=rid, dma_engine_mask=topo.mask(core, dst))
        sent += 16

    inc = []
    for s in range(n):
        if s == me:
            continue
        f = sum(counts[t][me] for t in range(s))
        for k, (a, c) in enumerate(pieces(counts[s][me])):
            inc.append((k, s, f + a, c))
    for k, s, f, c in sorted(inc):
        q = next_queue()
        q.wait_ge(T.sem["arr%d_%d" % (s, k)], 16)
        q.dma_start(T.y[:, f:f + c], T.land[:, f:f + c]).then_inc(T.sem.stored, 16)
        stores += 1

    if sent:
        g.wait_ge(T.sem.sent, sent)
    if stores:
        g.wait_ge(T.sem.stored, 16 * stores)
